import numpy as np
import ml_dtypes


def mxq(x, axis, fmt="e4m3"):
    dtype, down = {"e4m3": (ml_dtypes.float8_e4m3fn, 7), "e5m2": (ml_dtypes.float8_e5m2, 14)}[fmt]
    v = np.moveaxis(np.asarray(x, np.float32).astype(ml_dtypes.bfloat16).astype(np.float64), axis, -1)
    blocks = v.reshape(v.shape[:-1] + (-1, 32))
    amax = np.abs(blocks).max(-1, keepdims=True)
    byte = np.maximum(np.where(amax > 0, np.frexp(amax)[1] - 1 + 127, 0) - down, 1)
    scale = np.exp2(byte - 127.0)
    codes = (blocks / scale).astype(np.float32).astype(dtype).astype(np.float64)
    return np.moveaxis((codes * scale).reshape(v.shape), -1, axis)


WIDE = False


def mx_kscale(k):
    if not WIDE:
        return np.ones(k)
    levels = np.array([10, -10, 5, -5, 0])
    if k % 512:
        return np.exp2(np.random.permutation(np.resize(levels, k // 32))).repeat(32)
    a = np.empty((k // 512, 16))
    for p in range(k // 512):
        a[p, :8] = np.random.permutation(np.resize(levels, 8))
        for g in range(8):
            far = levels[np.abs(levels - a[p, g]) >= 10]
            a[p, g + 8] = far[np.random.randint(len(far))]
    return np.exp2(a.ravel()).repeat(32)


def f64(x):
    return np.asarray(x).astype(np.float64)


def striped(idx):
    return np.tile(np.asarray(idx).reshape(-1, 16).T, (8, 1)).astype(np.uint16)


def unstriped(offs):
    return offs[:16].T.reshape(-1).astype(np.int64)


B, N, T, D, DV, NQ = 1, 512, 2048, 512, 256, 256


def setup_inputs():
    n = np.random.standard_normal
    idx = np.sort(np.random.permutation(T)[:B * N].reshape(B, N), axis=1).reshape(-1)
    s = mx_kscale(D)[:, None]
    u = np.ones(T)
    u[idx] = mx_kscale(B * N)
    r = np.random.uniform(0.5, 2.0, T)
    k = n((D, T)) / s
    v = n((DV, T)) / (u * r)
    when = np.zeros(T)
    when[idx] = np.sort(np.random.permutation(2 * N)[:B * N])
    return {
        "qT": (n((B, D, NQ)) * s * (1.00 / np.sqrt(D))).astype(np.float32),
        "kT": k.astype(np.float32),
        "vT": v.astype(np.float32),
        "vs": np.tile(u * r, (128, 1)).astype(np.float32),
        "pos": np.tile(when, (128, 1)).astype(np.float32),
        "slope": np.exp2(-np.random.randint(8, 13, (B, NQ, 1))).astype(np.float32),
        "sink": (2.0 + 3.0 * n((B, NQ, 1))).astype(np.float32),
        "offs": striped(idx),
    }


def reference(qT, kT, vT, vs, pos, slope, sink, offs):
    idx = unstriped(offs)
    k = f64(kT)
    v = f64(vT)
    pick = lambda x: x[:, idx].reshape(x.shape[0], B, N).transpose(1, 0, 2)
    q = f64(qT)
    score = mxq(q, 1, "e4m3").transpose(0, 2, 1) @ mxq(pick(k), 1, "e4m3")
    score = score + f64(slope) * pick(f64(pos))[:, :1, :]
    m = np.maximum(score.max(-1, keepdims=True), f64(sink))
    p = np.exp(score - m)
    total = p.sum(-1, keepdims=True) + np.exp(f64(sink) - m)
    w = p * pick(f64(vs))[:, :1, :]
    y = mxq(w, 2, "e4m3") @ mxq(pick(v).transpose(0, 2, 1), 1, "e4m3")
    y = y / total
    return y

@@ -1,0 +1,194 @@
+from contextlib import ExitStack
+
+import concourse.mybir as mybir
+from concourse.masks import make_identity
+
+F32 = mybir.dt.float32
+BF16 = mybir.dt.bfloat16
+U32 = mybir.dt.uint32
+U16 = mybir.dt.uint16
+U8 = mybir.dt.uint8
+FP8X4 = mybir.dt.float8_e4m3fn_x4
+ACT = mybir.ActivationFunctionType
+ALU = mybir.AluOpType
+
+P = 128
+D, NQ, N, T, DV = 512, 256, 512, 2048, 256
+QB = NQ // P
+VB = DV // P
+FLOPS = 2 * NQ * N * (D + DV)
+BYTES = 4 * (D * NQ + D * T + DV * T + 2 * T + 2 * NQ + NQ * DV) + 2 * P * (N // 16)
+
+
+def tile_attend_x_alibi_sink_srt_kernel(tc, qT, kT, vT, vs, pos, slope, sink, offs, out):
+    nc = tc.nc
+    with ExitStack() as ctx:
+        keep = ctx.enter_context(tc.tile_pool(name="keep", bufs=1))
+        psum = ctx.enter_context(tc.psum_pool(name="psum", bufs=1))
+
+        offsets = keep.tile([P, N // 16], U16, name="offsets")
+        nc.sync.dma_start(offsets[:], offs)
+
+        k_raw = [keep.tile([P, T], F32, name=f"k_raw{t}") for t in range(4)]
+        q_raw = keep.tile([P, 4, NQ], F32, name="q_raw")
+        v_raw = [keep.tile([P, T], F32, name=f"v_raw{b}") for b in range(VB)]
+        rows = keep.tile([P, P], F32, name="rows")
+        pos_raw = keep.tile([P, T], F32, name="pos_raw")
+        vs_raw = keep.tile([P, T], F32, name="vs_raw")
+        k_planes = kT.rearrange("(p t) n -> p t n", t=4)
+        for t in (0, 1):
+            nc.sync.dma_start(k_raw[t][:], k_planes[:, t, :])
+
+        warm = keep.tile([P, 1], F32, name="warm")
+        nc.vector.memset(warm[:], 0.0)
+        nc.scalar.activation(warm[:], warm[:], ACT.Exp)
+
+        nc.vector.memset(rows[:], 0.0)
+        nc.sync.dma_start(rows[0:2, :], slope.rearrange("o (b p) x -> (o b) (p x)", p=P))
+        nc.sync.dma_start(rows[2:4, :], sink.rearrange("o (b p) x -> (o b) (p x)", p=P))
+        nc.vector.memset(pos_raw[:], 0.0)
+        nc.sync.dma_start(pos_raw[0:1, :], pos[0:1, :])
+        nc.vector.memset(vs_raw[:], 0.0)
+        nc.sync.dma_start(vs_raw[0:1, :], vs[0:1, :])
+        for t in (2, 3):
+            nc.sync.dma_start(k_raw[t][:], k_planes[:, t, :])
+        nc.sync.dma_start(q_raw[:], qT.rearrange("o (p t) n -> p (o t) n", t=4))
+        for b in range(VB):
+            nc.sync.dma_start(v_raw[b][:], vT[b * P : (b + 1) * P, :])
+
+        ident = keep.tile([P, P], F32, name="ident")
+        make_identity(nc, ident[:])
+        ident_bf = keep.tile([P, P], BF16, name="ident_bf")
+        nc.gpsimd.tensor_copy(ident_bf[:], ident[:])
+
+        k_bf = keep.tile([P, N, 4], BF16, align_bytes=64, name="k_bf")
+        for t in (0, 1):
+            nc.vector.tensor_copy(k_bf[:, :, t], k_raw[t][:].indirect(offsets[:]))
+
+        s = [keep.tile([P, N + 4], F32, name=f"s{b}") for b in range(QB)]
+        cols_ps = psum.tile([P, P], F32, tag="y0", name="cols_ps")
+        nc.tensor.transpose(cols_ps[:], rows[:], ident[:])
+        slope_col = keep.tile([P, QB], F32, name="slope_col")
+        nc.scalar.copy(slope_col[:], cols_ps[:, 0:QB])
+        for b in range(QB):
+            nc.scalar.copy(s[b][:, N : N + 1], cols_ps[:, QB + b : QB + b + 1])
+
+        pos_g = keep.tile([P, N], F32, name="pos_g")
+        nc.vector.tensor_copy(pos_g[:], pos_raw[:].indirect(offsets[:]))
+        posT_ps = psum.tile([P, 4, P], F32, tag="p0", name="posT_ps")
+        for t in range(4):
+            nc.tensor.transpose(posT_ps[:, t, :], pos_g[:, t::4], ident[:])
+        posT = keep.tile([P, 4], F32, name="posT")
+        nc.scalar.copy(posT[:], posT_ps[:, :, 0])
+        posb_ps = psum.tile([P, 4, P], F32, tag="p1", name="posb_ps")
+        for t in range(4):
+            nc.tensor.transpose(posb_ps[:, t, :], posT[:, t : t + 1].to_broadcast([P, P]), ident[:])
+        posb = keep.tile([P, 4, P], F32, name="posb")
+        nc.scalar.copy(posb[:], posb_ps[:])
+
+        vs_g = keep.tile([P, N], F32, name="vs_g")
+        nc.vector.tensor_copy(vs_g[:], vs_raw[:].indirect(offsets[:]))
+        vsT_ps = psum.tile([P, 4, P], F32, tag="v0", name="vsT_ps")
+        for t in range(4):
+            nc.tensor.transpose(vsT_ps[:, t, :], vs_g[:, t::4], ident[:])
+        vsT = keep.tile([P, 4], F32, name="vsT")
+        nc.scalar.copy(vsT[:], vsT_ps[:, :, 0])
+
+        q_in = [keep.tile([P, P, 4], BF16, align_bytes=64, name=f"q_in{b}") for b in range(QB)]
+        q_codes = [keep.tile([P, P], U32, align_bytes=64, name=f"q_codes{b}") for b in range(QB)]
+        q_scales = [keep.tile([P, P], U8, align_bytes=64, name=f"q_scales{b}") for b in range(QB)]
+        k_codes = keep.tile([P, N], U32, align_bytes=64, name="k_codes")
+        k_scales = keep.tile([P, N], U8, align_bytes=64, name="k_scales")
+        nc.vector.tensor_copy(k_bf[:, :, 2], k_raw[2][:].indirect(offsets[:]))
+        nc.vector.tensor_copy(k_bf[:, :, 3], k_raw[3][:].indirect(offsets[:]))
+        for b in range(QB):
+            nc.scalar.copy(q_in[b][:], q_raw[:, :, b * P : (b + 1) * P].rearrange("p t n -> p n t"))
+        nc.vector.quantize_mx(out=k_codes[:].bitcast(FP8X4), scales=k_scales[:], in_=k_bf[:].rearrange("p n t -> p (n t)"))
+        for b in range(QB):
+            nc.vector.quantize_mx(out=q_codes[b][:].bitcast(FP8X4), scales=q_scales[b][:], in_=q_in[b][:].rearrange("p n t -> p (n t)"))
+
+        scores = [psum.tile([P, N], F32, tag=f"s{b}", name=f"scores{b}") for b in range(QB)]
+        for b in range(QB):
+            nc.tensor.matmul_mx(
+                out=scores[b][:],
+                lhsT=q_codes[b][:].bitcast(FP8X4),
+                lhsT_scale=q_scales[b][:],
+                rhs=k_codes[:].bitcast(FP8X4),
+                rhs_scale=k_scales[:],
+                start=True,
+                stop=True,
+            )
+
+        v_bf = [keep.tile([P, 4, P], BF16, name=f"v_bf{b}") for b in range(VB)]
+        v_in = keep.tile([P, DV, 4], BF16, align_bytes=64, name="v_in")
+        v_codes = keep.tile([P, DV], U32, align_bytes=64, name="v_codes")
+        v_scales = keep.tile([P, DV], U8, align_bytes=64, name="v_scales")
+
+        def gather_values(b):
+            nc.vector.tensor_copy(v_bf[b][:].rearrange("p t m -> p m t"), v_raw[b][:].indirect(offsets[:]))
+
+        def turn_values(b):
+            ps = psum.tile([P, 4, P], BF16, tag=f"v{b}", name=f"v_ps{b}")
+            for t in range(4):
+                nc.tensor.transpose(ps[:, t, :], v_bf[b][:, t, :], ident_bf[:])
+            nc.scalar.copy(v_in[:, b * P : (b + 1) * P, :], ps[:].rearrange("m t e -> m e t"))
+
+        neg_max = [keep.tile([P, 1], F32, name=f"neg_max{b}") for b in range(QB)]
+        total = [keep.tile([P, 1], F32, name=f"total{b}") for b in range(QB)]
+        inv = [keep.tile([P, 1], F32, name=f"inv{b}") for b in range(QB)]
+        p = [keep.tile([P, N + 4], F32, name=f"p{b}") for b in range(QB)]
+        w_in = [keep.tile([P, P, 4], BF16, align_bytes=64, name=f"w_in{b}") for b in range(QB)]
+        w_codes = [keep.tile([P, P], U32, align_bytes=64, name=f"w_codes{b}") for b in range(QB)]
+        w_scales = [keep.tile([P, P], U8, align_bytes=64, name=f"w_scales{b}") for b in range(QB)]
+        y_sb = [keep.tile([P, DV], F32, name=f"y_sb{b}") for b in range(QB)]
+
+        def softmax(b):
+            nc.vector.scalar_tensor_tensor(
+                s[b][:, 0:N].rearrange("q (t m) -> q t m", t=4),
+                posb[:],
+                slope_col[:, b : b + 1],
+                scores[b][:].rearrange("q (m t) -> q t m", t=4),
+                ALU.mult,
+                ALU.add,
+            )
+            nc.vector.tensor_reduce(neg_max[b][:], s[b][:, 0 : N + 1], mybir.AxisListType.X, ALU.max, negate=True)
+            nc.scalar.activation(p[b][:, 0 : N + 1], s[b][:, 0 : N + 1], ACT.Exp, bias=neg_max[b][:], accum_out=total[b][:])
+
+        def turn_weights(b):
+            ps = psum.tile([P, 4, P], F32, tag=f"p{b}", name=f"p_ps{b}")
+            for t in range(4):
+                nc.tensor.transpose(ps[:, t, :], p[b][:, t * P : (t + 1) * P], ident[:])
+            nc.vector.tensor_tensor(
+                w_in[b][:],
+                ps[:].rearrange("m t q -> m q t"),
+                vsT[:].unsqueeze(1).to_broadcast([P, P, 4]),
+                ALU.mult,
+            )
+            nc.vector.quantize_mx(out=w_codes[b][:].bitcast(FP8X4), scales=w_scales[b][:], in_=w_in[b][:].rearrange("m q t -> m (q t)"))
+            nc.vector.reciprocal(inv[b][:], total[b][:])
+
+        def finish(b):
+            y = psum.tile([P, DV], F32, tag=f"y{b}", name=f"y{b}")
+            nc.tensor.matmul_mx(
+                out=y[:],
+                lhsT=w_codes[b][:].bitcast(FP8X4),
+                lhsT_scale=w_scales[b][:],
+                rhs=v_codes[:].bitcast(FP8X4),
+                rhs_scale=v_scales[:],
+                start=True,
+                stop=True,
+            )
+            nc.scalar.activation(y_sb[b][:], y[:], ACT.Copy, scale=inv[b][:])
+            nc.sync.dma_start(out[0, b * P : (b + 1) * P, :], y_sb[b][:])
+
+        softmax(0)
+        softmax(1)
+        gather_values(0)
+        turn_values(0)
+        gather_values(1)
+        turn_weights(0)
+        turn_values(1)
+        nc.vector.quantize_mx(out=v_codes[:].bitcast(FP8X4), scales=v_scales[:], in_=v_in[:].rearrange("m e t -> m (e t)"))
+        finish(0)
+        turn_weights(1)
+        finish(1)

@@ -142,7 +142,7 @@ def tile_attend_x_alibi_sink_srt_kernel(tc, qT, kT, vT, vs, pos, slope, sink, of
         w_scales = [keep.tile([P, P], U8, align_bytes=64, name=f"w_scales{b}") for b in range(QB)]
         y_sb = [keep.tile([P, DV], F32, name=f"y_sb{b}") for b in range(QB)]
 
-        def softmax(b):
+        def add_bias(b):
             nc.vector.scalar_tensor_tensor(
                 s[b][:, 0:N].rearrange("q (t m) -> q t m", t=4),
                 posb[:],
@@ -151,6 +151,8 @@ def tile_attend_x_alibi_sink_srt_kernel(tc, qT, kT, vT, vs, pos, slope, sink, of
                 ALU.mult,
                 ALU.add,
             )
+
+        def softmax(b):
             nc.vector.tensor_reduce(neg_max[b][:], s[b][:, 0 : N + 1], mybir.AxisListType.X, ALU.max, negate=True)
             nc.scalar.activation(p[b][:, 0 : N + 1], s[b][:, 0 : N + 1], ACT.Exp, bias=neg_max[b][:], accum_out=total[b][:])
 
@@ -164,23 +166,35 @@ def tile_attend_x_alibi_sink_srt_kernel(tc, qT, kT, vT, vs, pos, slope, sink, of
                 vsT[:].unsqueeze(1).to_broadcast([P, P, 4]),
                 ALU.mult,
             )
-            nc.vector.quantize_mx(out=w_codes[b][:].bitcast(FP8X4), scales=w_scales[b][:], in_=w_in[b][:].rearrange("m q t -> m (q t)"))
-            nc.vector.reciprocal(inv[b][:], total[b][:])
 
-        def finish(b):
-            y = psum.tile([P, DV], F32, tag=f"y{b}", name=f"y{b}")
+        def quantise_weights(b):
+            nc.vector.quantize_mx(out=w_codes[b][:].bitcast(FP8X4), scales=w_scales[b][:], in_=w_in[b][:].rearrange("m q t -> m (q t)"))
+
+        def quantise_values(b):
+            es = slice(b * P, (b + 1) * P)
+            nc.vector.quantize_mx(out=v_codes[:, es].bitcast(FP8X4), scales=v_scales[:, es], in_=v_in[:, es, :].rearrange("m e t -> m (e t)"))
+
+        y = [psum.tile([P, DV], F32, tag=f"y{b}", name=f"y{b}") for b in range(QB)]
+
+        def product(b, v):
+            es = slice(v * P, (v + 1) * P)
             nc.tensor.matmul_mx(
-                out=y[:],
+                out=y[b][:, es],
                 lhsT=w_codes[b][:].bitcast(FP8X4),
                 lhsT_scale=w_scales[b][:],
-                rhs=v_codes[:].bitcast(FP8X4),
-                rhs_scale=v_scales[:],
+                rhs=v_codes[:, es].bitcast(FP8X4),
+                rhs_scale=v_scales[:, es],
                 start=True,
                 stop=True,
             )
-            nc.scalar.activation(y_sb[b][:], y[:], ACT.Copy, scale=inv[b][:])
+
+        def finish(b):
+            nc.vector.reciprocal(inv[b][:], total[b][:])
+            nc.scalar.activation(y_sb[b][:], y[b][:], ACT.Copy, scale=inv[b][:])
             nc.sync.dma_start(out[0, b * P : (b + 1) * P, :], y_sb[b][:])
 
+        add_bias(0)
+        add_bias(1)
         softmax(0)
         softmax(1)
         gather_values(0)
@@ -188,7 +202,14 @@ def tile_attend_x_alibi_sink_srt_kernel(tc, qT, kT, vT, vs, pos, slope, sink, of
         gather_values(1)
         turn_weights(0)
         turn_values(1)
-        nc.vector.quantize_mx(out=v_codes[:].bitcast(FP8X4), scales=v_scales[:], in_=v_in[:].rearrange("m e t -> m (e t)"))
-        finish(0)
         turn_weights(1)
+        quantise_values(0)
+        quantise_weights(0)
+        product(0, 0)
+        quantise_weights(1)
+        product(1, 0)
+        quantise_values(1)
+        product(0, 1)
+        product(1, 1)
+        finish(0)
         finish(1)

@@ -27,8 +27,6 @@ def tile_attend_x_alibi_sink_srt_kernel(tc, qT, kT, vT, vs, pos, slope, sink, of
         psum = ctx.enter_context(tc.psum_pool(name="psum", bufs=1))
 
         offsets = keep.tile([P, N // 16], U16, name="offsets")
-        nc.sync.dma_start(offsets[:], offs)
-
         k_raw = [keep.tile([P, T], F32, name=f"k_raw{t}") for t in range(4)]
         q_raw = keep.tile([P, 4, NQ], F32, name="q_raw")
         v_raw = [keep.tile([P, T], F32, name=f"v_raw{b}") for b in range(VB)]
@@ -36,8 +34,9 @@ def tile_attend_x_alibi_sink_srt_kernel(tc, qT, kT, vT, vs, pos, slope, sink, of
         pos_raw = keep.tile([P, T], F32, name="pos_raw")
         vs_raw = keep.tile([P, T], F32, name="vs_raw")
         k_planes = kT.rearrange("(p t) n -> p t n", t=4)
-        for t in (0, 1):
-            nc.sync.dma_start(k_raw[t][:], k_planes[:, t, :])
+        nc.sync.dma_start(k_raw[0][:], k_planes[:, 0, :])
+        nc.sync.dma_start(offsets[:], offs)
+        nc.sync.dma_start(k_raw[1][:], k_planes[:, 1, :])
 
         warm = keep.tile([P, 1], F32, name="warm")
         nc.vector.memset(warm[:], 0.0)
@@ -66,7 +65,7 @@ def tile_attend_x_alibi_sink_srt_kernel(tc, qT, kT, vT, vs, pos, slope, sink, of
             nc.vector.tensor_copy(k_bf[:, :, t], k_raw[t][:].indirect(offsets[:]))
 
         s = [keep.tile([P, N + 4], F32, name=f"s{b}") for b in range(QB)]
-        cols_ps = psum.tile([P, P], F32, tag="y0", name="cols_ps")
+        cols_ps = psum.tile([P, P], F32, tag="s00", name="cols_ps")
         nc.tensor.transpose(cols_ps[:], rows[:], ident[:])
         slope_col = keep.tile([P, QB], F32, name="slope_col")
         nc.scalar.copy(slope_col[:], cols_ps[:, 0:QB])
@@ -100,24 +99,36 @@ def tile_attend_x_alibi_sink_srt_kernel(tc, qT, kT, vT, vs, pos, slope, sink, of
         k_codes = keep.tile([P, N], U32, align_bytes=64, name="k_codes")
         k_scales = keep.tile([P, N], U8, align_bytes=64, name="k_scales")
         nc.vector.tensor_copy(k_bf[:, :, 2], k_raw[2][:].indirect(offsets[:]))
-        nc.vector.tensor_copy(k_bf[:, :, 3], k_raw[3][:].indirect(offsets[:]))
+        H = N // 2
+        for h in range(2):
+            nc.vector.tensor_copy(
+                k_bf[:, h * H : (h + 1) * H, 3], k_raw[3][:].indirect(offsets[:, h * H // 16 : (h + 1) * H // 16])
+            )
         for b in range(QB):
             nc.scalar.copy(q_in[b][:], q_raw[:, :, b * P : (b + 1) * P].rearrange("p t n -> p n t"))
-        nc.vector.quantize_mx(out=k_codes[:].bitcast(FP8X4), scales=k_scales[:], in_=k_bf[:].rearrange("p n t -> p (n t)"))
+        for h in range(2):
+            ks = slice(h * H, (h + 1) * H)
+            nc.vector.quantize_mx(
+                out=k_codes[:, ks].bitcast(FP8X4),
+                scales=k_scales[:, ks],
+                in_=k_bf[:, ks, :].rearrange("p n t -> p (n t)"),
+            )
         for b in range(QB):
             nc.vector.quantize_mx(out=q_codes[b][:].bitcast(FP8X4), scales=q_scales[b][:], in_=q_in[b][:].rearrange("p n t -> p (n t)"))
 
-        scores = [psum.tile([P, N], F32, tag=f"s{b}", name=f"scores{b}") for b in range(QB)]
+        scores = [[psum.tile([P, H], F32, tag=f"s{b}{h}", name=f"scores{b}{h}") for h in range(2)] for b in range(QB)]
         for b in range(QB):
-            nc.tensor.matmul_mx(
-                out=scores[b][:],
-                lhsT=q_codes[b][:].bitcast(FP8X4),
-                lhsT_scale=q_scales[b][:],
-                rhs=k_codes[:].bitcast(FP8X4),
-                rhs_scale=k_scales[:],
-                start=True,
-                stop=True,
-            )
+            for h in range(2):
+                ks = slice(h * H, (h + 1) * H)
+                nc.tensor.matmul_mx(
+                    out=scores[b][h][:],
+                    lhsT=q_codes[b][:].bitcast(FP8X4),
+                    lhsT_scale=q_scales[b][:],
+                    rhs=k_codes[:, ks].bitcast(FP8X4),
+                    rhs_scale=k_scales[:, ks],
+                    start=True,
+                    stop=True,
+                )
 
         v_bf = [keep.tile([P, 4, P], BF16, name=f"v_bf{b}") for b in range(VB)]
         v_in = keep.tile([P, DV, 4], BF16, align_bytes=64, name="v_in")
@@ -143,14 +154,16 @@ def tile_attend_x_alibi_sink_srt_kernel(tc, qT, kT, vT, vs, pos, slope, sink, of
         y_sb = [keep.tile([P, DV], F32, name=f"y_sb{b}") for b in range(QB)]
 
         def add_bias(b):
-            nc.vector.scalar_tensor_tensor(
-                s[b][:, 0:N].rearrange("q (t m) -> q t m", t=4),
-                posb[:],
-                slope_col[:, b : b + 1],
-                scores[b][:].rearrange("q (m t) -> q t m", t=4),
-                ALU.mult,
-                ALU.add,
-            )
+            for h in range(2):
+                ms = slice(h * P // 2, (h + 1) * P // 2)
+                nc.vector.scalar_tensor_tensor(
+                    s[b][:, 0:N].rearrange("q (t m) -> q t m", t=4)[:, :, ms],
+                    posb[:, :, ms],
+                    slope_col[:, b : b + 1],
+                    scores[b][h][:].rearrange("q (m t) -> q t m", t=4),
+                    ALU.mult,
+                    ALU.add,
+                )
 
         def softmax(b):
             nc.vector.tensor_reduce(neg_max[b][:], s[b][:, 0 : N + 1], mybir.AxisListType.X, ALU.max, negate=True)
@@ -174,12 +187,12 @@ def tile_attend_x_alibi_sink_srt_kernel(tc, qT, kT, vT, vs, pos, slope, sink, of
             es = slice(b * P, (b + 1) * P)
             nc.vector.quantize_mx(out=v_codes[:, es].bitcast(FP8X4), scales=v_scales[:, es], in_=v_in[:, es, :].rearrange("m e t -> m (e t)"))
 
-        y = [psum.tile([P, DV], F32, tag=f"y{b}", name=f"y{b}") for b in range(QB)]
+        y = [[psum.tile([P, P], F32, tag=f"s{b}{v}", name=f"y{b}{v}") for v in range(VB)] for b in range(QB)]
 
         def product(b, v):
             es = slice(v * P, (v + 1) * P)
             nc.tensor.matmul_mx(
-                out=y[b][:, es],
+                out=y[b][v][:],
                 lhsT=w_codes[b][:].bitcast(FP8X4),
                 lhsT_scale=w_scales[b][:],
                 rhs=v_codes[:, es].bitcast(FP8X4),
@@ -189,14 +202,20 @@ def tile_attend_x_alibi_sink_srt_kernel(tc, qT, kT, vT, vs, pos, slope, sink, of
             )
 
         def finish(b):
-            nc.vector.reciprocal(inv[b][:], total[b][:])
-            nc.scalar.activation(y_sb[b][:], y[b][:], ACT.Copy, scale=inv[b][:])
+            for v in range(VB):
+                es = slice(v * P, (v + 1) * P)
+                if b == 0 or v == 0:
+                    nc.scalar.activation(y_sb[b][:, es], y[b][v][:], ACT.Copy, scale=inv[b][:])
+                else:
+                    nc.vector.tensor_scalar(y_sb[b][:, es], y[b][v][:], inv[b][:], None, ALU.mult)
             nc.sync.dma_start(out[0, b * P : (b + 1) * P, :], y_sb[b][:])
 
         add_bias(0)
         add_bias(1)
         softmax(0)
         softmax(1)
+        for b in range(QB):
+            nc.vector.reciprocal(inv[b][:], total[b][:])
         gather_values(0)
         turn_values(0)
         gather_values(1)

from contextlib import ExitStack

import concourse.mybir as mybir
from concourse.masks import make_identity

F32 = mybir.dt.float32
BF16 = mybir.dt.bfloat16
U32 = mybir.dt.uint32
U16 = mybir.dt.uint16
U8 = mybir.dt.uint8
FP8X4 = mybir.dt.float8_e4m3fn_x4
ACT = mybir.ActivationFunctionType
ALU = mybir.AluOpType

P = 128
D, NQ, N, T, DV = 512, 256, 512, 2048, 256
QB = NQ // P
VB = DV // P
FLOPS = 2 * NQ * N * (D + DV)
BYTES = 4 * (D * NQ + D * T + DV * T + 2 * T + 2 * NQ + NQ * DV) + 2 * P * (N // 16)


def tile_attend_x_alibi_sink_srt_kernel(tc, qT, kT, vT, vs, pos, slope, sink, offs, out):
    nc = tc.nc
    with ExitStack() as ctx:
        keep = ctx.enter_context(tc.tile_pool(name="keep", bufs=1))
        psum = ctx.enter_context(tc.psum_pool(name="psum", bufs=1))

        offsets = keep.tile([P, N // 16], U16, name="offsets")
        k_raw = [keep.tile([P, T], F32, name=f"k_raw{t}") for t in range(4)]
        q_raw = keep.tile([P, 4, NQ], F32, name="q_raw")
        v_raw = [keep.tile([P, T], F32, name=f"v_raw{b}") for b in range(VB)]
        rows = keep.tile([P, P], F32, name="rows")
        pos_raw = keep.tile([P, T], F32, name="pos_raw")
        vs_raw = keep.tile([P, T], F32, name="vs_raw")
        k_planes = kT.rearrange("(p t) n -> p t n", t=4)
        nc.sync.dma_start(k_raw[0][:], k_planes[:, 0, :])
        nc.sync.dma_start(offsets[:], offs)
        nc.sync.dma_start(k_raw[1][:], k_planes[:, 1, :])

        warm = keep.tile([P, 1], F32, name="warm")
        nc.vector.memset(warm[:], 0.0)
        nc.scalar.activation(warm[:], warm[:], ACT.Exp)

        nc.vector.memset(rows[:], 0.0)
        nc.sync.dma_start(rows[0:2, :], slope.rearrange("o (b p) x -> (o b) (p x)", p=P))
        nc.sync.dma_start(rows[2:4, :], sink.rearrange("o (b p) x -> (o b) (p x)", p=P))
        nc.vector.memset(pos_raw[:], 0.0)
        nc.sync.dma_start(pos_raw[0:1, :], pos[0:1, :])
        nc.vector.memset(vs_raw[:], 0.0)
        nc.sync.dma_start(vs_raw[0:1, :], vs[0:1, :])
        for t in (2, 3):
            nc.sync.dma_start(k_raw[t][:], k_planes[:, t, :])
        nc.sync.dma_start(q_raw[:], qT.rearrange("o (p t) n -> p (o t) n", t=4))
        for b in range(VB):
            nc.sync.dma_start(v_raw[b][:], vT[b * P : (b + 1) * P, :])

        ident = keep.tile([P, P], F32, name="ident")
        make_identity(nc, ident[:])
        ident_bf = keep.tile([P, P], BF16, name="ident_bf")
        nc.gpsimd.tensor_copy(ident_bf[:], ident[:])

        k_bf = keep.tile([P, N, 4], BF16, align_bytes=64, name="k_bf")
        for t in (0, 1):
            nc.vector.tensor_copy(k_bf[:, :, t], k_raw[t][:].indirect(offsets[:]))

        s = [keep.tile([P, N + 4], F32, name=f"s{b}") for b in range(QB)]
        cols_ps = psum.tile([P, P], F32, tag="s00", name="cols_ps")
        nc.tensor.transpose(cols_ps[:], rows[:], ident[:])
        slope_col = keep.tile([P, QB], F32, name="slope_col")
        nc.scalar.copy(slope_col[:], cols_ps[:, 0:QB])
        for b in range(QB):
            nc.scalar.copy(s[b][:, N : N + 1], cols_ps[:, QB + b : QB + b + 1])

        pos_g = keep.tile([P, N], F32, name="pos_g")
        nc.vector.tensor_copy(pos_g[:], pos_raw[:].indirect(offsets[:]))
        posT_ps = psum.tile([P, 4, P], F32, tag="p0", name="posT_ps")
        for t in range(4):
            nc.tensor.transpose(posT_ps[:, t, :], pos_g[:, t::4], ident[:])
        posT = keep.tile([P, 4], F32, name="posT")
        nc.scalar.copy(posT[:], posT_ps[:, :, 0])
        posb_ps = psum.tile([P, 4, P], F32, tag="p1", name="posb_ps")
        for t in range(4):
            nc.tensor.transpose(posb_ps[:, t, :], posT[:, t : t + 1].to_broadcast([P, P]), ident[:])
        posb = keep.tile([P, 4, P], F32, name="posb")
        nc.scalar.copy(posb[:], posb_ps[:])

        vs_g = keep.tile([P, N], F32, name="vs_g")
        nc.vector.tensor_copy(vs_g[:], vs_raw[:].indirect(offsets[:]))
        vsT_ps = psum.tile([P, 4, P], F32, tag="v0", name="vsT_ps")
        for t in range(4):
            nc.tensor.transpose(vsT_ps[:, t, :], vs_g[:, t::4], ident[:])
        vsT = keep.tile([P, 4], F32, name="vsT")
        nc.scalar.copy(vsT[:], vsT_ps[:, :, 0])

        q_in = [keep.tile([P, P, 4], BF16, align_bytes=64, name=f"q_in{b}") for b in range(QB)]
        q_codes = [keep.tile([P, P], U32, align_bytes=64, name=f"q_codes{b}") for b in range(QB)]
        q_scales = [keep.tile([P, P], U8, align_bytes=64, name=f"q_scales{b}") for b in range(QB)]
        k_codes = keep.tile([P, N], U32, align_bytes=64, name="k_codes")
        k_scales = keep.tile([P, N], U8, align_bytes=64, name="k_scales")
        nc.vector.tensor_copy(k_bf[:, :, 2], k_raw[2][:].indirect(offsets[:]))
        H = N // 2
        for h in range(2):
            nc.vector.tensor_copy(
                k_bf[:, h * H : (h + 1) * H, 3], k_raw[3][:].indirect(offsets[:, h * H // 16 : (h + 1) * H // 16])
            )
        for b in range(QB):
            nc.scalar.copy(q_in[b][:], q_raw[:, :, b * P : (b + 1) * P].rearrange("p t n -> p n t"))
        for h in range(2):
            ks = slice(h * H, (h + 1) * H)
            nc.vector.quantize_mx(
                out=k_codes[:, ks].bitcast(FP8X4),
                scales=k_scales[:, ks],
                in_=k_bf[:, ks, :].rearrange("p n t -> p (n t)"),
            )
        for b in range(QB):
            nc.vector.quantize_mx(out=q_codes[b][:].bitcast(FP8X4), scales=q_scales[b][:], in_=q_in[b][:].rearrange("p n t -> p (n t)"))

        scores = [[psum.tile([P, H], F32, tag=f"s{b}{h}", name=f"scores{b}{h}") for h in range(2)] for b in range(QB)]
        for b in range(QB):
            for h in range(2):
                ks = slice(h * H, (h + 1) * H)
                nc.tensor.matmul_mx(
                    out=scores[b][h][:],
                    lhsT=q_codes[b][:].bitcast(FP8X4),
                    lhsT_scale=q_scales[b][:],
                    rhs=k_codes[:, ks].bitcast(FP8X4),
                    rhs_scale=k_scales[:, ks],
                    start=True,
                    stop=True,
                )

        v_bf = [keep.tile([P, 4, P], BF16, name=f"v_bf{b}") for b in range(VB)]
        v_in = keep.tile([P, DV, 4], BF16, align_bytes=64, name="v_in")
        v_codes = keep.tile([P, DV], U32, align_bytes=64, name="v_codes")
        v_scales = keep.tile([P, DV], U8, align_bytes=64, name="v_scales")

        def gather_values(b):
            nc.vector.tensor_copy(v_bf[b][:].rearrange("p t m -> p m t"), v_raw[b][:].indirect(offsets[:]))

        def turn_values(b):
            ps = psum.tile([P, 4, P], BF16, tag=f"v{b}", name=f"v_ps{b}")
            for t in range(4):
                nc.tensor.transpose(ps[:, t, :], v_bf[b][:, t, :], ident_bf[:])
            nc.scalar.copy(v_in[:, b * P : (b + 1) * P, :], ps[:].rearrange("m t e -> m e t"))

        neg_max = [keep.tile([P, 1], F32, name=f"neg_max{b}") for b in range(QB)]
        total = [keep.tile([P, 1], F32, name=f"total{b}") for b in range(QB)]
        inv = [keep.tile([P, 1], F32, name=f"inv{b}") for b in range(QB)]
        p = [keep.tile([P, N + 4], F32, name=f"p{b}") for b in range(QB)]
        w_in = [keep.tile([P, P, 4], BF16, align_bytes=64, name=f"w_in{b}") for b in range(QB)]
        w_codes = [keep.tile([P, P], U32, align_bytes=64, name=f"w_codes{b}") for b in range(QB)]
        w_scales = [keep.tile([P, P], U8, align_bytes=64, name=f"w_scales{b}") for b in range(QB)]
        y_sb = [keep.tile([P, DV], F32, name=f"y_sb{b}") for b in range(QB)]

        def add_bias(b):
            for h in range(2):
                ms = slice(h * P // 2, (h + 1) * P // 2)
                nc.vector.scalar_tensor_tensor(
                    s[b][:, 0:N].rearrange("q (t m) -> q t m", t=4)[:, :, ms],
                    posb[:, :, ms],
                    slope_col[:, b : b + 1],
                    scores[b][h][:].rearrange("q (m t) -> q t m", t=4),
                    ALU.mult,
                    ALU.add,
                )

        def softmax(b):
            nc.vector.tensor_reduce(neg_max[b][:], s[b][:, 0 : N + 1], mybir.AxisListType.X, ALU.max, negate=True)
            nc.scalar.activation(p[b][:, 0 : N + 1], s[b][:, 0 : N + 1], ACT.Exp, bias=neg_max[b][:], accum_out=total[b][:])

        def turn_weights(b):
            ps = psum.tile([P, 4, P], F32, tag=f"p{b}", name=f"p_ps{b}")
            for t in range(4):
                nc.tensor.transpose(ps[:, t, :], p[b][:, t * P : (t + 1) * P], ident[:])
            nc.vector.tensor_tensor(
                w_in[b][:],
                ps[:].rearrange("m t q -> m q t"),
                vsT[:].unsqueeze(1).to_broadcast([P, P, 4]),
                ALU.mult,
            )

        def quantise_weights(b):
            nc.vector.quantize_mx(out=w_codes[b][:].bitcast(FP8X4), scales=w_scales[b][:], in_=w_in[b][:].rearrange("m q t -> m (q t)"))

        def quantise_values(b):
            es = slice(b * P, (b + 1) * P)
            nc.vector.quantize_mx(out=v_codes[:, es].bitcast(FP8X4), scales=v_scales[:, es], in_=v_in[:, es, :].rearrange("m e t -> m (e t)"))

        y = [[psum.tile([P, P], F32, tag=f"s{b}{v}", name=f"y{b}{v}") for v in range(VB)] for b in range(QB)]

        def product(b, v):
            es = slice(v * P, (v + 1) * P)
            nc.tensor.matmul_mx(
                out=y[b][v][:],
                lhsT=w_codes[b][:].bitcast(FP8X4),
                lhsT_scale=w_scales[b][:],
                rhs=v_codes[:, es].bitcast(FP8X4),
                rhs_scale=v_scales[:, es],
                start=True,
                stop=True,
            )

        def finish(b):
            for v in range(VB):
                es = slice(v * P, (v + 1) * P)
                if b == 0 or v == 0:
                    nc.scalar.activation(y_sb[b][:, es], y[b][v][:], ACT.Copy, scale=inv[b][:])
                else:
                    nc.vector.tensor_scalar(y_sb[b][:, es], y[b][v][:], inv[b][:], None, ALU.mult)
            nc.sync.dma_start(out[0, b * P : (b + 1) * P, :], y_sb[b][:])

        add_bias(0)
        add_bias(1)
        softmax(0)
        softmax(1)
        for b in range(QB):
            nc.vector.reciprocal(inv[b][:], total[b][:])
        gather_values(0)
        turn_values(0)
        gather_values(1)
        turn_weights(0)
        turn_values(1)
        turn_weights(1)
        quantise_values(0)
        quantise_weights(0)
        product(0, 0)
        quantise_weights(1)
        product(1, 0)
        quantise_values(1)
        product(0, 1)
        product(1, 1)
        finish(0)
        finish(1)
